import numpy as np
import ml_dtypes


def mxq(x, axis, fmt="e4m3"):
    dtype, down = {"e4m3": (ml_dtypes.float8_e4m3fn, 7), "e5m2": (ml_dtypes.float8_e5m2, 14)}[fmt]
    v = np.moveaxis(np.asarray(x, np.float32).astype(ml_dtypes.bfloat16).astype(np.float64), axis, -1)
    blocks = v.reshape(v.shape[:-1] + (-1, 32))
    amax = np.abs(blocks).max(-1, keepdims=True)
    byte = np.maximum(np.where(amax > 0, np.frexp(amax)[1] - 1 + 127, 0) - down, 1)
    scale = np.exp2(byte - 127.0)
    codes = (blocks / scale).astype(np.float32).astype(dtype).astype(np.float64)
    return np.moveaxis((codes * scale).reshape(v.shape), -1, axis)


WIDE = False


def mx_kscale(k):
    if not WIDE:
        return np.ones(k)
    levels = np.array([10, -10, 5, -5, 0])
    if k % 512:
        return np.exp2(np.random.permutation(np.resize(levels, k // 32))).repeat(32)
    a = np.empty((k // 512, 16))
    for p in range(k // 512):
        a[p, :8] = np.random.permutation(np.resize(levels, 8))
        for g in range(8):
            far = levels[np.abs(levels - a[p, g]) >= 10]
            a[p, g + 8] = far[np.random.randint(len(far))]
    return np.exp2(a.ravel()).repeat(32)


def f64(x):
    return np.asarray(x).astype(np.float64)


def striped(idx):
    return np.tile(idx.reshape(-1, 16).T, (8, 1)).astype(np.uint16)


def unstriped(offs):
    return offs[:16].T.reshape(-1).astype(np.int64)


E2M1 = np.array([0.0, 0.5, 1.0, 1.5, 2.0, 3.0, 4.0, 6.0, -0.0, -0.5, -1.0, -1.5, -2.0, -3.0, -4.0, -6.0])


def pack_fp4(w):
    k, n = w.shape
    w = f64(np.asarray(w, np.float32).astype(ml_dtypes.bfloat16)).reshape(k // 32, 32, n)
    amax = np.abs(w).max(1)
    mant, ex = np.frexp(amax / 6.0)
    byte = np.clip(np.where(amax > 0, np.where(mant > 0.5, ex, ex - 1) + 127, 1), 1, 254)
    scaled = (w * np.exp2(127.0 - byte)[:, None, :]).reshape(k, n).astype(np.float32)
    c = np.ascontiguousarray(scaled.reshape(k // 512, 128, 4, n).transpose(0, 1, 3, 2)).astype(ml_dtypes.float4_e2m1fn).view(np.uint8) & 0xF
    words = (c[..., 0::2] | (c[..., 1::2] << 4)).reshape(k // 512, 128, 2 * n)
    return np.ascontiguousarray(words), np.ascontiguousarray(byte.astype(np.uint8).reshape(k // 512, 16, n))


def unpack_fp4(words, scales):
    g, _, n = scales.shape
    words = np.ascontiguousarray(words).reshape(g, 128, n, 2)
    nib = np.empty((g, 128, n, 4), np.uint8)
    nib[..., 0::2] = words & 0xF
    nib[..., 1::2] = words >> 4
    vals = E2M1[nib] * np.repeat(np.exp2(scales.astype(np.float64) - 127.0), 8, axis=1)[..., None]
    return vals.transpose(0, 1, 3, 2).reshape(g * 512, n)


def relu(v):
    return np.maximum(v, 0.0)


K, T, S, D, V, H, N, U = 512, 2048, 512, 4, 512, 512, 128, 1024
P = 2 ** 7


def setup_inputs():
    n = np.random.standard_normal
    s = mx_kscale(K)[:, None]
    u = mx_kscale(H)
    packed_xT = pack_fp4(n((K, T)) * s)
    return {
        "x_words": packed_xT[0],
        "x_scales": packed_xT[1],
        "w1": (n((K, H)) / np.sqrt(K) / s * u).astype(np.float32),
        "w2": (n((H, N)) / np.sqrt(H) / u[:, None]).astype(np.float32),
        "gate": np.tile(np.random.uniform(0.2, 0.6, (D, 1, V)), (1, P, 1)).astype(np.float32),
        "emb": (0.5 * n((H, U)) * u[:, None]).astype(np.float32),
        "offs": striped(np.random.permutation(T)[:S]),
        "cell": striped(np.random.permutation(U)[:S]),
        "pos1": striped(np.random.permutation(U)[:V]),
        "pos2": striped(np.random.permutation(U)[:V]),
        "pos3": striped(np.random.permutation(U)[:V]),
        "pos4": striped(np.random.permutation(U)[:V]),
    }


def reference(x_words, x_scales, w1, w2, gate, emb, offs, cell, pos1, pos2, pos3, pos4):
    xq = unpack_fp4(x_words, x_scales)[:, unstriped(offs)]
    up = np.zeros((H, U))
    up[:, unstriped(cell)] = relu(mxq(f64(w1), 0, "e4m3").T @ xq)
    z = up + f64(emb)
    y = relu(mxq(f64(w2), 0, "e4m3").T @ mxq(z, 0, "e4m3"))
    return y[:, unstriped(pos1)] * f64(gate)[0, :1] + y[:, unstriped(pos2)] * f64(gate)[1, :1] + y[:, unstriped(pos3)] * f64(gate)[2, :1] + y[:, unstriped(pos4)] * f64(gate)[3, :1]

@@ -1,0 +1,163 @@
+from contextlib import ExitStack
+
+import concourse.mybir as mybir
+
+K, T, S, D, V, H, N, U = 512, 2048, 512, 4, 512, 512, 128, 1024
+FLOPS = 2 * K * H * S + 2 * H * N * U
+
+F32 = mybir.dt.float32
+BF16 = mybir.dt.bfloat16
+I32 = mybir.dt.int32
+U32 = mybir.dt.uint32
+U16 = mybir.dt.uint16
+U8 = mybir.dt.uint8
+FP8X4 = mybir.dt.float8_e4m3fn_x4
+FP4X4 = mybir.dt.float4_e2m1fn_x4
+RELU = mybir.ActivationFunctionType.Relu
+ADD = mybir.AluOpType.add
+MULT = mybir.AluOpType.mult
+
+P = 128
+PACK = 4
+RUN = 8
+CHUNK = 256
+HALF = S // 2
+
+
+def tile_picked_devox_relu_p_kernel(tc, x_words, x_scales, w1, w2, gate, emb, offs, cell, pos1, pos2, pos3, pos4, out):
+    nc = tc.nc
+    with ExitStack() as ctx:
+        lists = ctx.enter_context(tc.tile_pool(name="lists", bufs=1))
+        sb = ctx.enter_context(tc.tile_pool(name="sb", bufs=1))
+        psum = ctx.enter_context(tc.psum_pool(name="psum", bufs=1))
+
+        def load_list(src, name):
+            t = lists.tile([P, S // 16], U16, name=name)
+            nc.sync.dma_start(t[:], src)
+            return t
+
+        xs_win = sb.tile([P, T], U8, name="xs_win", align_bytes=64)
+        nc.vector.memset(xs_win[:].bitcast(I32), 0)
+        up = [sb.tile([P, U], F32, name="up%d" % t, align_bytes=64) for t in range(PACK)]
+        for t in range(PACK):
+            nc.gpsimd.memset(up[t][:], 0.0)
+
+        offs_t = load_list(offs, "offs_t")
+        xw_win = sb.tile([P, T], U16, name="xw_win", align_bytes=64)
+        nc.sync.dma_start(xw_win[:].bitcast(I32), x_words[0].bitcast(I32))
+        for q in range(4):
+            nc.sync.dma_start(xs_win[32 * q : 32 * q + 4, :].bitcast(I32), x_scales[0, 4 * q : 4 * q + 4, :].bitcast(I32))
+        w1_v = w1.rearrange("(p j) c -> p j c", j=PACK)
+        w1_raw = [sb.tile([P, PACK, H // 2], F32, name="w1_raw%d" % a, align_bytes=64) for a in range(2)]
+        for a in range(2):
+            nc.sync.dma_start(w1_raw[a][:], w1_v[:, :, a * (H // 2) : (a + 1) * (H // 2)])
+        cell_t = load_list(cell, "cell_t")
+        w2_v = w2.rearrange("(b t r) n -> t b r n", t=PACK, r=RUN)
+        w2_raw = sb.tile([P, PACK, N], F32, name="w2_raw", align_bytes=64)
+        for t in range(PACK):
+            nc.sync.dma_start(w2_raw[:, t, :], w2_v[t])
+        emb_v = emb.rearrange("(b t r) c -> t b r c", t=PACK, r=RUN)
+        emb_t = [sb.tile([P, U], F32, name="emb%d" % t, align_bytes=64) for t in range(PACK)]
+        for t in range(PACK):
+            nc.sync.dma_start(emb_t[t][:], emb_v[t])
+        pos_t = [load_list(src, "pos%d_t" % d) for d, src in enumerate((pos1, pos2, pos3, pos4))]
+        gate_t = sb.tile([P, D, V], F32, name="gate_t", align_bytes=64)
+        nc.sync.dma_start(gate_t[:], gate.rearrange("d p v -> p d v"))
+
+        xw = sb.tile([P, S], U16, name="xw", align_bytes=64)
+        xs = sb.tile([P, S], U8, name="xs", align_bytes=64)
+        nc.vector.tensor_copy(xw[:], xw_win[:].indirect(offs_t[:]))
+        nc.vector.tensor_copy(xs[:], xs_win[:].indirect(offs_t[:]))
+
+        w1_b = [sb.tile([P, P * PACK], BF16, name="w1_b%d" % t, align_bytes=64) for t in range(PACK)]
+        w1_c = [sb.tile([P, P], U32, name="w1_c%d" % t, align_bytes=64) for t in range(PACK)]
+        w1_s = [sb.tile([P, P], U8, name="w1_s%d" % t, align_bytes=64) for t in range(PACK)]
+
+        def w1_views(t, a):
+            dst = w1_b[t][:, a * 256 : (a + 1) * 256].rearrange("p (b r j) -> p b r j", r=RUN, j=PACK)
+            src = w1_raw[a][:].rearrange("p j (b t r) -> p t b r j", t=PACK, r=RUN)[:, t]
+            return dst, src
+
+        for t in range(PACK):
+            nc.scalar.copy(*w1_views(t, 0))
+        for t in range(PACK):
+            nc.vector.tensor_copy(*w1_views(t, 1))
+        for t in range(PACK):
+            nc.vector.quantize_mx(out=w1_c[t][:].bitcast(FP8X4), scales=w1_s[t][:], in_=w1_b[t][:])
+
+        h_ps = [psum.tile([P, S], F32, name="h_ps%d" % t) for t in range(PACK)]
+        h = [sb.tile([P, S], F32, name="h%d" % t, align_bytes=64) for t in range(PACK)]
+        pieces = [(0, 0, HALF), (1, 0, HALF), (0, HALF, S), (1, HALF, S), (2, 0, S), (3, 0, S)]
+        banks = [0, 1, 2, 3, 0, 1]
+        for (t, a, b), bank in zip(pieces, banks):
+            nc.tensor.matmul_mx(out=h_ps[bank][:, a:b], lhsT=w1_c[t][:].bitcast(FP8X4), lhsT_scale=w1_s[t][:],
+                                rhs=xw[:, a:b].bitcast(FP4X4), rhs_scale=xs[:, a:b], start=True, stop=True)
+            nc.scalar.activation(h[t][:, a:b], h_ps[bank][:, a:b], RELU)
+
+        w2_b = sb.tile([P, N * PACK], BF16, name="w2_b", align_bytes=64)
+        w2_c = sb.tile([P, N], U32, name="w2_c", align_bytes=64)
+        w2_s = sb.tile([P, N], U8, name="w2_s", align_bytes=64)
+        nc.scalar.copy(w2_b[:].rearrange("p (n t) -> p n t", t=PACK), w2_raw[:].rearrange("p t n -> p n t"))
+        nc.vector.quantize_mx(out=w2_c[:].bitcast(FP8X4), scales=w2_s[:], in_=w2_b[:])
+
+        chunks = U // CHUNK
+        z01 = sb.tile([P, 2, U], BF16, name="z01", align_bytes=64)
+        z23 = [sb.tile([P, 2, CHUNK], BF16, name="z23_%d" % c, align_bytes=64) for c in range(chunks)]
+        zi = [sb.tile([P, CHUNK, PACK], BF16, name="zi%d" % c, align_bytes=64) for c in range(chunks)]
+        z_c = [sb.tile([P, CHUNK], U32, name="z_c%d" % c, align_bytes=64) for c in range(chunks)]
+        z_s = [sb.tile([P, CHUNK], U8, name="z_s%d" % c, align_bytes=64) for c in range(chunks)]
+
+        def cols(c):
+            return slice(c * CHUNK, (c + 1) * CHUNK)
+
+        for t, a, b in pieces:
+            nc.vector.tensor_copy(up[t][:].indirect(cell_t[:, a // 16 : b // 16]), h[t][:, a:b])
+            if b == S and t < 2:
+                nc.gpsimd.tensor_tensor(z01[:, t, :], up[t][:], emb_t[t][:], ADD)
+            if b == S and t == 1:
+                for c in range(chunks):
+                    nc.scalar.copy(zi[c][:, :, 0:2], z01[:, :, cols(c)].rearrange("p e c -> p c e"))
+            if t == 2:
+                for c in range(chunks):
+                    nc.gpsimd.tensor_tensor(z23[c][:, 0, :], up[2][:, cols(c)], emb_t[2][:, cols(c)], ADD)
+
+        def add3(c):
+            nc.vector.tensor_tensor(z23[c][:, 1, :], up[3][:, cols(c)], emb_t[3][:, cols(c)], ADD)
+
+        def place(c, copy):
+            copy(zi[c][:, :, 2:4], z23[c][:].rearrange("p e c -> p c e"))
+
+        y = sb.tile([P, U], F32, name="y", align_bytes=64)
+        y_ps = [psum.tile([P, CHUNK], F32, name="y_ps%d" % c) for c in range(chunks)]
+
+        def second(c):
+            nc.vector.quantize_mx(out=z_c[c][:].bitcast(FP8X4), scales=z_s[c][:], in_=zi[c][:].rearrange("p c t -> p (c t)"))
+            nc.tensor.matmul_mx(out=y_ps[c][:], lhsT=w2_c[:].bitcast(FP8X4), lhsT_scale=w2_s[:],
+                                rhs=z_c[c][:].bitcast(FP8X4), rhs_scale=z_s[c][:], start=True, stop=True)
+
+        add3(0)
+        add3(1)
+        place(0, nc.scalar.copy)
+        add3(2)
+        place(1, nc.vector.tensor_copy)
+        place(2, nc.scalar.copy)
+        add3(3)
+        second(0)
+        second(1)
+        place(3, nc.vector.tensor_copy)
+        second(2)
+        second(3)
+        for c in range(chunks):
+            nc.scalar.activation(y[:, cols(c)], y_ps[c][:], RELU)
+
+        prod = sb.tile([P, D, V], F32, name="prod", align_bytes=64)
+        s01 = sb.tile([P, V], F32, name="s01", align_bytes=64)
+        s012 = sb.tile([P, V], F32, name="s012", align_bytes=64)
+        res = sb.tile([P, V], F32, name="res", align_bytes=64)
+        for d in range(D):
+            nc.vector.tensor_tensor(prod[:, d, :], y[:].indirect(pos_t[d][:]), gate_t[:, d, :], MULT)
+            if d == 2:
+                nc.vector.tensor_tensor(s01[:], prod[:, 0, :], prod[:, 1, :], ADD)
+        nc.vector.tensor_tensor(s012[:], s01[:], prod[:, 2, :], ADD)
+        nc.vector.tensor_tensor(res[:], s012[:], prod[:, 3, :], ADD)
+        nc.sync.dma_start(out, res[:])

@@ -1,6 +1,7 @@
 from contextlib import ExitStack
 
 import concourse.mybir as mybir
+from concourse.masks import make_identity
 
 K, T, S, D, V, H, N, U = 512, 2048, 512, 4, 512, 512, 128, 1024
 FLOPS = 2 * K * H * S + 2 * H * N * U
@@ -13,15 +14,16 @@ U16 = mybir.dt.uint16
 U8 = mybir.dt.uint8
 FP8X4 = mybir.dt.float8_e4m3fn_x4
 FP4X4 = mybir.dt.float4_e2m1fn_x4
+COPY = mybir.ActivationFunctionType.Copy
 RELU = mybir.ActivationFunctionType.Relu
 ADD = mybir.AluOpType.add
 MULT = mybir.AluOpType.mult
 
 P = 128
 PACK = 4
-RUN = 8
 CHUNK = 256
-HALF = S // 2
+VA = 384
+VB = V - VA
 
 
 def tile_picked_devox_relu_p_kernel(tc, x_words, x_scales, w1, w2, gate, emb, offs, cell, pos1, pos2, pos3, pos4, out):
@@ -31,133 +33,235 @@ def tile_picked_devox_relu_p_kernel(tc, x_words, x_scales, w1, w2, gate, emb, of
         sb = ctx.enter_context(tc.tile_pool(name="sb", bufs=1))
         psum = ctx.enter_context(tc.psum_pool(name="psum", bufs=1))
 
+        def sbuf(shape, dtype, name):
+            return sb.tile(shape, dtype, name=name, align_bytes=64)
+
+        def bank(b, shape, dtype, name):
+            return psum.tile(shape, dtype, name=name, tag="bank%d" % b)
+
         def load_list(src, name):
             t = lists.tile([P, S // 16], U16, name=name)
             nc.sync.dma_start(t[:], src)
             return t
 
-        xs_win = sb.tile([P, T], U8, name="xs_win", align_bytes=64)
-        nc.vector.memset(xs_win[:].bitcast(I32), 0)
-        up = [sb.tile([P, U], F32, name="up%d" % t, align_bytes=64) for t in range(PACK)]
-        for t in range(PACK):
-            nc.gpsimd.memset(up[t][:], 0.0)
-
-        offs_t = load_list(offs, "offs_t")
-        xw_win = sb.tile([P, T], U16, name="xw_win", align_bytes=64)
-        nc.sync.dma_start(xw_win[:].bitcast(I32), x_words[0].bitcast(I32))
-        for q in range(4):
-            nc.sync.dma_start(xs_win[32 * q : 32 * q + 4, :].bitcast(I32), x_scales[0, 4 * q : 4 * q + 4, :].bitcast(I32))
-        w1_v = w1.rearrange("(p j) c -> p j c", j=PACK)
-        w1_raw = [sb.tile([P, PACK, H // 2], F32, name="w1_raw%d" % a, align_bytes=64) for a in range(2)]
-        for a in range(2):
-            nc.sync.dma_start(w1_raw[a][:], w1_v[:, :, a * (H // 2) : (a + 1) * (H // 2)])
-        cell_t = load_list(cell, "cell_t")
-        w2_v = w2.rearrange("(b t r) n -> t b r n", t=PACK, r=RUN)
-        w2_raw = sb.tile([P, PACK, N], F32, name="w2_raw", align_bytes=64)
-        for t in range(PACK):
-            nc.sync.dma_start(w2_raw[:, t, :], w2_v[t])
-        emb_v = emb.rearrange("(b t r) c -> t b r c", t=PACK, r=RUN)
-        emb_t = [sb.tile([P, U], F32, name="emb%d" % t, align_bytes=64) for t in range(PACK)]
-        for t in range(PACK):
-            nc.sync.dma_start(emb_t[t][:], emb_v[t])
-        pos_t = [load_list(src, "pos%d_t" % d) for d, src in enumerate((pos1, pos2, pos3, pos4))]
-        gate_t = sb.tile([P, D, V], F32, name="gate_t", align_bytes=64)
-        nc.sync.dma_start(gate_t[:], gate.rearrange("d p v -> p d v"))
-
-        xw = sb.tile([P, S], U16, name="xw", align_bytes=64)
-        xs = sb.tile([P, S], U8, name="xs", align_bytes=64)
-        nc.vector.tensor_copy(xw[:], xw_win[:].indirect(offs_t[:]))
-        nc.vector.tensor_copy(xs[:], xs_win[:].indirect(offs_t[:]))
-
-        w1_b = [sb.tile([P, P * PACK], BF16, name="w1_b%d" % t, align_bytes=64) for t in range(PACK)]
-        w1_c = [sb.tile([P, P], U32, name="w1_c%d" % t, align_bytes=64) for t in range(PACK)]
-        w1_s = [sb.tile([P, P], U8, name="w1_s%d" % t, align_bytes=64) for t in range(PACK)]
-
-        def w1_views(t, a):
-            dst = w1_b[t][:, a * 256 : (a + 1) * 256].rearrange("p (b r j) -> p b r j", r=RUN, j=PACK)
-            src = w1_raw[a][:].rearrange("p j (b t r) -> p t b r j", t=PACK, r=RUN)[:, t]
-            return dst, src
-
-        for t in range(PACK):
-            nc.scalar.copy(*w1_views(t, 0))
-        for t in range(PACK):
-            nc.vector.tensor_copy(*w1_views(t, 1))
-        for t in range(PACK):
-            nc.vector.quantize_mx(out=w1_c[t][:].bitcast(FP8X4), scales=w1_s[t][:], in_=w1_b[t][:])
-
-        h_ps = [psum.tile([P, S], F32, name="h_ps%d" % t) for t in range(PACK)]
-        h = [sb.tile([P, S], F32, name="h%d" % t, align_bytes=64) for t in range(PACK)]
-        pieces = [(0, 0, HALF), (1, 0, HALF), (0, HALF, S), (1, HALF, S), (2, 0, S), (3, 0, S)]
-        banks = [0, 1, 2, 3, 0, 1]
-        for (t, a, b), bank in zip(pieces, banks):
-            nc.tensor.matmul_mx(out=h_ps[bank][:, a:b], lhsT=w1_c[t][:].bitcast(FP8X4), lhsT_scale=w1_s[t][:],
-                                rhs=xw[:, a:b].bitcast(FP4X4), rhs_scale=xs[:, a:b], start=True, stop=True)
-            nc.scalar.activation(h[t][:, a:b], h_ps[bank][:, a:b], RELU)
-
-        w2_b = sb.tile([P, N * PACK], BF16, name="w2_b", align_bytes=64)
-        w2_c = sb.tile([P, N], U32, name="w2_c", align_bytes=64)
-        w2_s = sb.tile([P, N], U8, name="w2_s", align_bytes=64)
-        nc.scalar.copy(w2_b[:].rearrange("p (n t) -> p n t", t=PACK), w2_raw[:].rearrange("p t n -> p n t"))
-        nc.vector.quantize_mx(out=w2_c[:].bitcast(FP8X4), scales=w2_s[:], in_=w2_b[:])
-
-        chunks = U // CHUNK
-        z01 = sb.tile([P, 2, U], BF16, name="z01", align_bytes=64)
-        z23 = [sb.tile([P, 2, CHUNK], BF16, name="z23_%d" % c, align_bytes=64) for c in range(chunks)]
-        zi = [sb.tile([P, CHUNK, PACK], BF16, name="zi%d" % c, align_bytes=64) for c in range(chunks)]
-        z_c = [sb.tile([P, CHUNK], U32, name="z_c%d" % c, align_bytes=64) for c in range(chunks)]
-        z_s = [sb.tile([P, CHUNK], U8, name="z_s%d" % c, align_bytes=64) for c in range(chunks)]
+        def blk(i):
+            return slice(i * P, (i + 1) * P)
 
         def cols(c):
             return slice(c * CHUNK, (c + 1) * CHUNK)
 
-        for t, a, b in pieces:
-            nc.vector.tensor_copy(up[t][:].indirect(cell_t[:, a // 16 : b // 16]), h[t][:, a:b])
-            if b == S and t < 2:
-                nc.gpsimd.tensor_tensor(z01[:, t, :], up[t][:], emb_t[t][:], ADD)
-            if b == S and t == 1:
-                for c in range(chunks):
-                    nc.scalar.copy(zi[c][:, :, 0:2], z01[:, :, cols(c)].rearrange("p e c -> p c e"))
-            if t == 2:
-                for c in range(chunks):
-                    nc.gpsimd.tensor_tensor(z23[c][:, 0, :], up[2][:, cols(c)], emb_t[2][:, cols(c)], ADD)
+        def quantize(name, src, width):
+            codes = sbuf([P, width], U32, name + "_c")
+            scales = sbuf([P, width], U8, name + "_s")
+            nc.vector.quantize_mx(out=codes[:].bitcast(FP8X4), scales=scales[:], in_=src)
+            return codes, scales
 
-        def add3(c):
-            nc.vector.tensor_tensor(z23[c][:, 1, :], up[3][:, cols(c)], emb_t[3][:, cols(c)], ADD)
+        xs_win = sbuf([P, T], U8, "xs_win")
+        nc.gpsimd.memset(xs_win[:].bitcast(I32), 0)
+        ident = sbuf([P, P], F32, "ident")
+        make_identity(nc, ident[:])
+        ident_b = sbuf([P, P], BF16, "ident_b")
+        make_identity(nc, ident_b[:])
+        up = [sbuf([P, U], F32, "up%d" % s) for s in range(PACK)]
+        for s in range(PACK):
+            (nc.vector if s < 2 else nc.gpsimd).memset(up[s][:], 0.0)
 
-        def place(c, copy):
+        def turn(dst, src, start, stop):
+            nc.tensor.matmul(dst, src, ident[:], start=start, stop=stop, is_transpose=True)
+
+        xw_win = sbuf([P, T], U16, "xw_win")
+        nc.sync.dma_start(xw_win[:].bitcast(I32), x_words[0].bitcast(I32))
+        offs_t = load_list(offs, "offs_t")
+        for q in range(4):
+            nc.sync.dma_start(xs_win[32 * q : 32 * q + 4, :].bitcast(I32), x_scales[0, 4 * q : 4 * q + 4, :].bitcast(I32))
+        w1_v = w1.rearrange("(p j) c -> p j c", j=PACK)
+        w1_raw = [sbuf([P, PACK, H // 2], F32, "w1_raw%d" % a) for a in range(2)]
+        for a in range(2):
+            nc.sync.dma_start(w1_raw[a][:], w1_v[:, :, a * (H // 2) : (a + 1) * (H // 2)])
+        cell_t = load_list(cell, "cell_t")
+        emb_lo = emb.rearrange("(a b h i) c -> h a b i c", a=2, h=2, i=16)[0]
+        emb_hi = emb.rearrange("(b g r) c -> g b r c", g=4, r=8)
+        emb_t = [sbuf([P, U], F32, "emb%d" % s) for s in range(PACK)]
+        w2_raw = sbuf([P, PACK, N], F32, "w2_raw")
+        for s in range(2):
+            nc.sync.dma_start(emb_t[s][:], emb_lo[s])
+        nc.sync.dma_start(w2_raw[:, 0:2, :].rearrange("p e n -> p (e n)"), w2.rearrange("(b h r e) n -> h b r (e n)", h=2, r=8, e=2)[0])
+        for s in range(2, PACK):
+            nc.sync.dma_start(w2_raw[:, s, :], w2.rearrange("(b g r) n -> g b r n", g=4, r=8)[s])
+        for s in range(2, PACK):
+            nc.sync.dma_start(emb_t[s][:], emb_hi[s])
+        pos_t = [load_list(src, "pos%d_t" % d) for d, src in enumerate((pos1, pos2, pos3, pos4))]
+        gate_a = sbuf([P, VA], F32, "gate_a")
+        nc.sync.dma_start(gate_a[:], gate[:, 0 : P // D, 0:VA].rearrange("d r v -> r d v"))
+        gate_b = sbuf([P, D, VB], F32, "gate_b")
+        nc.sync.dma_start(gate_b[:], gate[:, :, VA:V].rearrange("d p v -> p d v"))
+
+        xw = sbuf([P, S], U16, "xw")
+        xs = sbuf([P, S], U8, "xs")
+        nc.vector.tensor_copy(xw[:], xw_win[:].indirect(offs_t[:]))
+        nc.vector.tensor_copy(xs[:], xs_win[:].indirect(offs_t[:]))
+
+        w1_b = [sbuf([P, P * PACK], BF16, "w1_b%d" % s) for s in range(PACK)]
+        h_ps = [bank(b, [P, S], F32, "h_ps%d" % b) for b in range(PACK)]
+        h = [sbuf([P, S], F32, "h%d" % s) for s in range(PACK)]
+
+        def cast_lo(s):
+            dst = w1_b[s][:].rearrange("p (b i j) -> p b i j", i=16, j=PACK)
+            src = w1_raw[s][:].rearrange("p j (b h i) -> p h b i j", h=2, i=16)[:, 0]
+            for half in range(2):
+                nc.scalar.copy(dst[:, 4 * half : 4 * half + 4], src[:, 4 * half : 4 * half + 4])
+
+        def cast_hi(s, a):
+            dst = w1_b[s][:, a * 256 : (a + 1) * 256].rearrange("p (b r j) -> p b r j", r=8, j=PACK)
+            nc.scalar.copy(dst, w1_raw[a][:].rearrange("p j (b g r) -> p g b r j", g=4, r=8)[:, s])
+
+        def first(w, s, b, lo, cuts):
+            start = lo
+            for hi in cuts:
+                nc.tensor.matmul_mx(out=h_ps[b][:, lo:hi], lhsT=w[0][:].bitcast(FP8X4), lhsT_scale=w[1][:],
+                                    rhs=xw[:, lo:hi].bitcast(FP4X4), rhs_scale=xs[:, lo:hi], start=True, stop=True)
+                lo = hi
+            nc.scalar.activation(h[s][:, start:lo], h_ps[b][:, start:lo], RELU)
+
+        def scatter(s, a, b):
+            nc.vector.tensor_copy(up[s][:].indirect(cell_t[:, a // 16 : b // 16]), h[s][:, a:b])
+
+        cast_lo(0)
+        w1_q = quantize("w1q0", w1_b[0][:], P)
+        first(w1_q, 0, 0, 0, [S // 2])
+        scatter(0, 0, S // 2)
+        cast_lo(1)
+        for s in range(2, PACK):
+            for a in range(2):
+                cast_hi(s, a)
+        rest = [quantize("w1q%d" % s, w1_b[s][:], P) for s in range(1, PACK)]
+        first(w1_q, 0, 1, S // 2, [S])
+        scatter(0, S // 2, S)
+        for s in range(1, PACK):
+            first(rest[s - 1], s, (2, 3, 0)[s - 1], 0, [S])
+        scatter(1, 0, S)
+
+        w2_b = sbuf([P, N * PACK], BF16, "w2_b")
+        nc.scalar.copy(w2_b[:].rearrange("p (n t) -> p n t", t=PACK), w2_raw[:].rearrange("p t n -> p n t"))
+        w2_q = quantize("w2q", w2_b[:], N)
+
+        chunks = U // CHUNK
+        z23 = [sbuf([P, 2, CHUNK], BF16, "z23_%d" % c) for c in range(chunks)]
+        zi = [sbuf([P, CHUNK, PACK], BF16, "zi%d" % c) for c in range(chunks)]
+
+        zt01 = [sbuf([P, 4, 2, P], BF16, "zt01_%d" % a) for a in range(2)]
+        t01 = [[bank(4 + 2 * s + a, [P, 4, P], F32, "t%d_%d" % (s, a)) for a in range(2)] for s in range(2)]
+
+        def turn_lo(s, src, start):
+            for a in range(2):
+                for i in range(4):
+                    turn(t01[s][a][:, i, :], src[:, blk(4 * a + i)], start and i == 0, not start and i == 3)
+
+        def leave_lo(s):
+            for a in range(2):
+                nc.scalar.copy(zt01[a][:, :, s, :], t01[s][a][:])
+
+        turn_lo(0, emb_t[0], True)
+        turn_lo(1, emb_t[1], True)
+        turn_lo(0, up[0], False)
+        g_ps = bank(1, [P, VA // P, P], F32, "g_ps")
+        for i in range(VA // P):
+            turn(g_ps[:, i, :], gate_a[:, blk(i)], True, True)
+        leave_lo(0)
+        gate_c = sbuf([P, VA // P, D], F32, "gate_c")
+        nc.scalar.copy(gate_c[:], g_ps[:, :, 0:D])
+        turn_lo(1, up[1], False)
+        scatter(2, 0, S)
+        leave_lo(1)
+        w01 = [bank(2 + a, [P, 2, CHUNK], F32, "w01_%d" % a) for a in range(2)]
+        for a in range(2):
+            words = zt01[a][:].rearrange("q i s p -> q (i s p)").bitcast(F32)
+            for i in range(4):
+                turn(w01[a][:, i // 2, blk(i % 2)], words[:, blk(i)], True, True)
+
+        def place01(c):
+            dst = zi[c][:].rearrange("p c t -> p (c t)").bitcast(F32).rearrange("p (c u) -> p c u", u=2)
+            nc.scalar.copy(dst, w01[c // 2][:, c % 2, :].unsqueeze(2).to_broadcast([P, CHUNK, 2]))
+
+        spans = ((2, 4), (4, 8))
+        t2 = [bank(7 - a, [P, (hi - lo) * P], F32, "t2_%d" % a) for a, (lo, hi) in enumerate(spans)]
+        place01(0)
+        place01(1)
+        for src, start in ((emb_t[2], True), (up[2], False)):
+            for a, (lo, hi) in enumerate(spans):
+                for i in range(lo, hi):
+                    turn(t2[a][:, blk(i - lo)], src[:, blk(i)], start and i == lo, not start and i == hi - 1)
+        scatter(3, 0, S)
+        zt2 = [sbuf([P, (hi - lo) * P], BF16, "zt2_%d" % a) for a, (lo, hi) in enumerate(spans)]
+        z2_ps = [bank(4 + a, [P, (hi - lo) * P], BF16, "z2_ps%d" % a) for a, (lo, hi) in enumerate(spans)]
+        place01(2)
+        for a in range(2):
+            nc.scalar.copy(zt2[a][:], t2[a][:])
+        for a, (lo, hi) in enumerate(spans):
+            for i in range(hi - lo):
+                nc.tensor.transpose(z2_ps[a][:, blk(i)], zt2[a][:, blk(i)], ident_b[:])
+        place01(3)
+        nc.scalar.copy(z23[1][:, 0, :], z2_ps[0][:])
+        for c in (2, 3):
+            nc.scalar.copy(z23[c][:, 0, :], z2_ps[1][:, cols(c - 2)])
+
+        def add(s, c):
+            nc.vector.tensor_tensor(z23[c][:, s - 2, :], up[s][:, cols(c)], emb_t[s][:, cols(c)], ADD)
+
+        def place23(c, copy):
             copy(zi[c][:, :, 2:4], z23[c][:].rearrange("p e c -> p c e"))
 
-        y = sb.tile([P, U], F32, name="y", align_bytes=64)
-        y_ps = [psum.tile([P, CHUNK], F32, name="y_ps%d" % c) for c in range(chunks)]
+        y = sbuf([P, U], F32, "y")
+        y_ps = [bank((5, 4, 2, 3)[c], [P, CHUNK], F32, "y_ps%d" % c) for c in range(chunks)]
 
         def second(c):
-            nc.vector.quantize_mx(out=z_c[c][:].bitcast(FP8X4), scales=z_s[c][:], in_=zi[c][:].rearrange("p c t -> p (c t)"))
-            nc.tensor.matmul_mx(out=y_ps[c][:], lhsT=w2_c[:].bitcast(FP8X4), lhsT_scale=w2_s[:],
-                                rhs=z_c[c][:].bitcast(FP8X4), rhs_scale=z_s[c][:], start=True, stop=True)
+            codes, scales = quantize("zq%d" % c, zi[c][:].rearrange("p c t -> p (c t)"), CHUNK)
+            nc.tensor.matmul_mx(out=y_ps[c][:], lhsT=w2_q[0][:].bitcast(FP8X4), lhsT_scale=w2_q[1][:],
+                                rhs=codes[:].bitcast(FP8X4), rhs_scale=scales[:], start=True, stop=True)
 
-        add3(0)
-        add3(1)
-        place(0, nc.scalar.copy)
-        add3(2)
-        place(1, nc.vector.tensor_copy)
-        place(2, nc.scalar.copy)
-        add3(3)
-        second(0)
-        second(1)
-        place(3, nc.vector.tensor_copy)
-        second(2)
-        second(3)
+        add(2, 0)
+        for c in (1, 2, 0, 3):
+            add(3, c)
+        place23(0, nc.vector.tensor_copy)
+        for c in range(1, chunks):
+            place23(c, nc.scalar.copy)
+        for c in range(chunks):
+            second(c)
         for c in range(chunks):
             nc.scalar.activation(y[:, cols(c)], y_ps[c][:], RELU)
 
-        prod = sb.tile([P, D, V], F32, name="prod", align_bytes=64)
-        s01 = sb.tile([P, V], F32, name="s01", align_bytes=64)
-        s012 = sb.tile([P, V], F32, name="s012", align_bytes=64)
-        res = sb.tile([P, V], F32, name="res", align_bytes=64)
+        nblk = VA // P
+        got = [sbuf([P, VA], F32, "got%d" % d) for d in range(D)]
+        scaled = [sbuf([P, VA], F32, "scaled%d" % d) for d in range(D)]
+        acc_ps = bank(6, [P, VA], F32, "acc_ps")
+
+        def back(d):
+            for i in range(nblk):
+                turn(acc_ps[:, blk(i)], scaled[d][:, blk(i)], d == 0 and i == 0, d == D - 1 and i == nblk - 1)
+
         for d in range(D):
-            nc.vector.tensor_tensor(prod[:, d, :], y[:].indirect(pos_t[d][:]), gate_t[:, d, :], MULT)
+            nc.vector.tensor_copy(got[d][:], y[:].indirect(pos_t[d][:, 0 : VA // 16]))
+            if d > 1:
+                back(d - 2)
+            got_ps = bank(4 + d % 2, [P, VA], F32, "got_ps%d" % d)
+            for i in range(nblk):
+                turn(got_ps[:, blk(i)], got[d][:, blk(i)], True, True)
+            for i in range(nblk):
+                nc.scalar.activation(scaled[d][:, blk(i)], got_ps[:, blk(i)], COPY, scale=gate_c[:, i, d : d + 1])
+        back(D - 2)
+        back(D - 1)
+        res_a = sbuf([P, VA], F32, "res_a")
+        nc.scalar.copy(res_a[:], acc_ps[:])
+        nc.sync.dma_start(out[:, 0:VA], res_a[:])
+
+        prod = sbuf([P, D, VB], F32, "prod")
+        s01 = sbuf([P, VB], F32, "s01")
+        s012 = sbuf([P, VB], F32, "s012")
+        res_b = sbuf([P, VB], F32, "res_b")
+        for d in range(D):
+            nc.vector.tensor_tensor(prod[:, d, :], y[:].indirect(pos_t[d][:, VA // 16 : V // 16]), gate_b[:, d, :], MULT)
             if d == 2:
                 nc.vector.tensor_tensor(s01[:], prod[:, 0, :], prod[:, 1, :], ADD)
         nc.vector.tensor_tensor(s012[:], s01[:], prod[:, 2, :], ADD)
-        nc.vector.tensor_tensor(res[:], s012[:], prod[:, 3, :], ADD)
-        nc.sync.dma_start(out, res[:])
+        nc.vector.tensor_tensor(res_b[:], s012[:], prod[:, 3, :], ADD)
+        nc.sync.dma_start(out[:, VA:V], res_b[:])

@@ -21,28 +21,32 @@ MULT = mybir.AluOpType.mult
 
 P = 128
 PACK = 4
+LIST = 16
 CHUNK = 256
-VA = 384
+CHUNKS = U // CHUNK
+VA = 3 * P
 VB = V - VA
 
 
-def tile_picked_devox_relu_p_kernel(tc, x_words, x_scales, w1, w2, gate, emb, offs, cell, pos1, pos2, pos3, pos4, out):
+def tile_picked_devox_relu_p_kernel(
+    tc, x_words, x_scales, w1, w2, gate, emb, offs, cell, pos1, pos2, pos3, pos4, out
+):
     nc = tc.nc
     with ExitStack() as ctx:
         lists = ctx.enter_context(tc.tile_pool(name="lists", bufs=1))
         sb = ctx.enter_context(tc.tile_pool(name="sb", bufs=1))
         psum = ctx.enter_context(tc.psum_pool(name="psum", bufs=1))
 
-        def sbuf(shape, dtype, name):
-            return sb.tile(shape, dtype, name=name, align_bytes=64)
+        def sbuf(shape, dtype, name, tag=None):
+            return sb.tile(shape, dtype, name=name, tag=tag or name, align_bytes=64)
 
         def bank(b, shape, dtype, name):
             return psum.tile(shape, dtype, name=name, tag="bank%d" % b)
 
         def load_list(src, name):
-            t = lists.tile([P, S // 16], U16, name=name)
-            nc.sync.dma_start(t[:], src)
-            return t
+            tile = lists.tile([P, S // LIST], U16, name=name)
+            nc.sync.dma_start(tile[:], src)
+            return tile
 
         def blk(i):
             return slice(i * P, (i + 1) * P)
@@ -50,8 +54,8 @@ def tile_picked_devox_relu_p_kernel(tc, x_words, x_scales, w1, w2, gate, emb, of
         def cols(c):
             return slice(c * CHUNK, (c + 1) * CHUNK)
 
-        def quantize(name, src, width):
-            codes = sbuf([P, width], U32, name + "_c")
+        def quantize(name, src, width, tag=None):
+            codes = sbuf([P, width], U32, name + "_c", tag)
             scales = sbuf([P, width], U8, name + "_s")
             nc.vector.quantize_mx(out=codes[:].bitcast(FP8X4), scales=scales[:], in_=src)
             return codes, scales
@@ -61,10 +65,11 @@ def tile_picked_devox_relu_p_kernel(tc, x_words, x_scales, w1, w2, gate, emb, of
         ident = sbuf([P, P], F32, "ident")
         make_identity(nc, ident[:])
         ident_b = sbuf([P, P], BF16, "ident_b")
-        make_identity(nc, ident_b[:])
+        nc.scalar.copy(ident_b[:], ident[:])
         up = [sbuf([P, U], F32, "up%d" % s) for s in range(PACK)]
-        for s in range(PACK):
-            (nc.vector if s < 2 else nc.gpsimd).memset(up[s][:], 0.0)
+        for s in range(PACK - 1):
+            nc.vector.memset(up[s][:], 0.0)
+        nc.scalar.copy(up[PACK - 1][:], up[0][:])
 
         def turn(dst, src, start, stop):
             nc.tensor.matmul(dst, src, ident[:], start=start, stop=stop, is_transpose=True)
@@ -73,26 +78,26 @@ def tile_picked_devox_relu_p_kernel(tc, x_words, x_scales, w1, w2, gate, emb, of
         nc.sync.dma_start(xw_win[:].bitcast(I32), x_words[0].bitcast(I32))
         offs_t = load_list(offs, "offs_t")
         for q in range(4):
-            nc.sync.dma_start(xs_win[32 * q : 32 * q + 4, :].bitcast(I32), x_scales[0, 4 * q : 4 * q + 4, :].bitcast(I32))
-        w1_v = w1.rearrange("(p j) c -> p j c", j=PACK)
+            nc.sync.dma_start(
+                xs_win[32 * q : 32 * q + 4, :].bitcast(I32), x_scales[0, 4 * q : 4 * q + 4, :].bitcast(I32)
+            )
+        w1_rows = w1.rearrange("(p t) c -> p t c", t=PACK)
         w1_raw = [sbuf([P, PACK, H // 2], F32, "w1_raw%d" % a) for a in range(2)]
         for a in range(2):
-            nc.sync.dma_start(w1_raw[a][:], w1_v[:, :, a * (H // 2) : (a + 1) * (H // 2)])
+            nc.sync.dma_start(w1_raw[a][:], w1_rows[:, :, a * (H // 2) : (a + 1) * (H // 2)])
         cell_t = load_list(cell, "cell_t")
-        emb_lo = emb.rearrange("(a b h i) c -> h a b i c", a=2, h=2, i=16)[0]
-        emb_hi = emb.rearrange("(b g r) c -> g b r c", g=4, r=8)
+        emb_even = emb.rearrange("(s q e) c -> e s q c", s=2, e=2)[0]
+        emb_fourth = emb.rearrange("(p f) c -> f p c", f=PACK)
         emb_t = [sbuf([P, U], F32, "emb%d" % s) for s in range(PACK)]
         w2_raw = sbuf([P, PACK, N], F32, "w2_raw")
         for s in range(2):
-            nc.sync.dma_start(emb_t[s][:], emb_lo[s])
-        nc.sync.dma_start(w2_raw[:, 0:2, :].rearrange("p e n -> p (e n)"), w2.rearrange("(b h r e) n -> h b r (e n)", h=2, r=8, e=2)[0])
+            nc.sync.dma_start(emb_t[s][:], emb_even[s])
+        nc.sync.dma_start(w2_raw[:], w2.rearrange("(p f) n -> p f n", f=PACK))
         for s in range(2, PACK):
-            nc.sync.dma_start(w2_raw[:, s, :], w2.rearrange("(b g r) n -> g b r n", g=4, r=8)[s])
-        for s in range(2, PACK):
-            nc.sync.dma_start(emb_t[s][:], emb_hi[s])
+            nc.sync.dma_start(emb_t[s][:], emb_fourth[2 * s - 3])
         pos_t = [load_list(src, "pos%d_t" % d) for d, src in enumerate((pos1, pos2, pos3, pos4))]
         gate_a = sbuf([P, VA], F32, "gate_a")
-        nc.sync.dma_start(gate_a[:], gate[:, 0 : P // D, 0:VA].rearrange("d r v -> r d v"))
+        nc.sync.dma_start(gate_a[:], gate.rearrange("d (r f) v -> f (d r) v", f=D)[0, :, 0:VA])
         gate_b = sbuf([P, D, VB], F32, "gate_b")
         nc.sync.dma_start(gate_b[:], gate[:, :, VA:V].rearrange("d p v -> p d v"))
 
@@ -101,167 +106,184 @@ def tile_picked_devox_relu_p_kernel(tc, x_words, x_scales, w1, w2, gate, emb, of
         nc.vector.tensor_copy(xw[:], xw_win[:].indirect(offs_t[:]))
         nc.vector.tensor_copy(xs[:], xs_win[:].indirect(offs_t[:]))
 
-        w1_b = [sbuf([P, P * PACK], BF16, "w1_b%d" % s) for s in range(PACK)]
+        w1_even = [sbuf([P, P * PACK], BF16, "w1_even%d" % s) for s in range(2)]
+        w1_odd = sbuf([P, 2, P * PACK], BF16, "w1_odd")
         h_ps = [bank(b, [P, S], F32, "h_ps%d" % b) for b in range(PACK)]
         h = [sbuf([P, S], F32, "h%d" % s) for s in range(PACK)]
 
-        def cast_lo(s):
-            dst = w1_b[s][:].rearrange("p (b i j) -> p b i j", i=16, j=PACK)
-            src = w1_raw[s][:].rearrange("p j (b h i) -> p h b i j", h=2, i=16)[:, 0]
-            for half in range(2):
-                nc.scalar.copy(dst[:, 4 * half : 4 * half + 4], src[:, 4 * half : 4 * half + 4])
+        def cast_even(s):
+            dst = w1_even[s][:].rearrange("p (q t) -> p q t", t=PACK)
+            src = w1_raw[s][:].rearrange("p t (q e) -> p e q t", e=2)[:, 0]
+            for q in (0, P // 2):
+                nc.scalar.copy(dst[:, q : q + P // 2], src[:, q : q + P // 2])
 
-        def cast_hi(s, a):
-            dst = w1_b[s][:, a * 256 : (a + 1) * 256].rearrange("p (b r j) -> p b r j", r=8, j=PACK)
-            nc.scalar.copy(dst, w1_raw[a][:].rearrange("p j (b g r) -> p g b r j", g=4, r=8)[:, s])
+        def cast_odd(a):
+            dst = w1_odd[:].rearrange("p s (m t) -> p m s t", t=PACK)[:, a * P // 2 : (a + 1) * P // 2]
+            src = w1_raw[a][:].rearrange("p t (m s e) -> p e m s t", s=2, e=2)[:, 1]
+            for m in (0, P // 4):
+                nc.scalar.copy(dst[:, m : m + P // 4], src[:, m : m + P // 4])
 
-        def first(w, s, b, lo, cuts):
-            start = lo
-            for hi in cuts:
-                nc.tensor.matmul_mx(out=h_ps[b][:, lo:hi], lhsT=w[0][:].bitcast(FP8X4), lhsT_scale=w[1][:],
-                                    rhs=xw[:, lo:hi].bitcast(FP4X4), rhs_scale=xs[:, lo:hi], start=True, stop=True)
-                lo = hi
-            nc.scalar.activation(h[s][:, start:lo], h_ps[b][:, start:lo], RELU)
+        def first_product(s, b, lo, hi):
+            codes, scales = w1_q[s]
+            nc.tensor.matmul_mx(
+                out=h_ps[b][:, lo:hi],
+                lhsT=codes.bitcast(FP8X4),
+                lhsT_scale=scales,
+                rhs=xw[:, lo:hi].bitcast(FP4X4),
+                rhs_scale=xs[:, lo:hi],
+                start=True,
+                stop=True,
+            )
+            nc.scalar.activation(h[s][:, lo:hi], h_ps[b][:, lo:hi], RELU)
 
-        def scatter(s, a, b):
-            nc.vector.tensor_copy(up[s][:].indirect(cell_t[:, a // 16 : b // 16]), h[s][:, a:b])
+        def scatter(s, lo, hi):
+            nc.vector.tensor_copy(up[s][:].indirect(cell_t[:, lo // LIST : hi // LIST]), h[s][:, lo:hi])
 
-        cast_lo(0)
-        w1_q = quantize("w1q0", w1_b[0][:], P)
-        first(w1_q, 0, 0, 0, [S // 2])
+        cast_even(0)
+        codes, scales = quantize("w1q0", w1_even[0][:], P)
+        w1_q = [(codes[:], scales[:])]
+        first_product(0, 0, 0, S // 2)
         scatter(0, 0, S // 2)
-        cast_lo(1)
-        for s in range(2, PACK):
-            for a in range(2):
-                cast_hi(s, a)
-        rest = [quantize("w1q%d" % s, w1_b[s][:], P) for s in range(1, PACK)]
-        first(w1_q, 0, 1, S // 2, [S])
+        cast_even(1)
+        for a in range(2):
+            cast_odd(a)
+        codes, scales = quantize("w1q1", w1_even[1][:], P)
+        w1_q.append((codes[:], scales[:]))
+        codes, scales = quantize("w1q23", w1_odd[:].rearrange("p s c -> p (s c)"), 2 * P)
+        w1_q.extend((codes[:, blk(s)], scales[:, blk(s)]) for s in range(2))
+        first_product(0, 1, S // 2, S)
         scatter(0, S // 2, S)
         for s in range(1, PACK):
-            first(rest[s - 1], s, (2, 3, 0)[s - 1], 0, [S])
+            first_product(s, (s + 1) % PACK, 0, S)
         scatter(1, 0, S)
 
         w2_b = sbuf([P, N * PACK], BF16, "w2_b")
-        nc.scalar.copy(w2_b[:].rearrange("p (n t) -> p n t", t=PACK), w2_raw[:].rearrange("p t n -> p n t"))
+        nc.scalar.copy(
+            w2_b[:].rearrange("p (n u e) -> p n u e", u=2, e=2), w2_raw[:].rearrange("p (e u) n -> p n u e", u=2)
+        )
         w2_q = quantize("w2q", w2_b[:], N)
 
-        chunks = U // CHUNK
-        z23 = [sbuf([P, 2, CHUNK], BF16, "z23_%d" % c) for c in range(chunks)]
-        zi = [sbuf([P, CHUNK, PACK], BF16, "zi%d" % c) for c in range(chunks)]
+        z_odd = [sbuf([P, 2, CHUNK], BF16, "z_odd%d" % c) for c in range(CHUNKS)]
+        zi = [sbuf([P, CHUNK, PACK], BF16, "zi%d" % c) for c in range(CHUNKS)]
 
-        zt01 = [sbuf([P, 4, 2, P], BF16, "zt01_%d" % a) for a in range(2)]
-        t01 = [[bank(4 + 2 * s + a, [P, 4, P], F32, "t%d_%d" % (s, a)) for a in range(2)] for s in range(2)]
+        even_ps = [[bank(4 + 2 * s + a, [P, 4, P], F32, "even_ps%d_%d" % (s, a)) for a in range(2)] for s in range(2)]
+        even_t = [sbuf([P, 4, 2, P], BF16, "even_t%d" % a) for a in range(2)]
 
-        def turn_lo(s, src, start):
+        def turn_even(s, src, opens):
             for a in range(2):
                 for i in range(4):
-                    turn(t01[s][a][:, i, :], src[:, blk(4 * a + i)], start and i == 0, not start and i == 3)
+                    turn(even_ps[s][a][:, i, :], src[:, blk(4 * a + i)], opens and i == 0, not opens and i == 3)
 
-        def leave_lo(s):
+        def round_even(s):
             for a in range(2):
-                nc.scalar.copy(zt01[a][:, :, s, :], t01[s][a][:])
+                nc.scalar.copy(even_t[a][:, :, s, :], even_ps[s][a][:])
 
-        turn_lo(0, emb_t[0], True)
-        turn_lo(1, emb_t[1], True)
-        turn_lo(0, up[0], False)
-        g_ps = bank(1, [P, VA // P, P], F32, "g_ps")
+        turn_even(0, emb_t[0], True)
+        turn_even(1, emb_t[1], True)
+        turn_even(0, up[0], False)
+        gate_ps = bank(1, [P, VA // P, P], F32, "gate_ps")
         for i in range(VA // P):
-            turn(g_ps[:, i, :], gate_a[:, blk(i)], True, True)
-        leave_lo(0)
+            turn(gate_ps[:, i, :], gate_a[:, blk(i)], True, True)
+        round_even(0)
         gate_c = sbuf([P, VA // P, D], F32, "gate_c")
-        nc.scalar.copy(gate_c[:], g_ps[:, :, 0:D])
-        turn_lo(1, up[1], False)
+        nc.scalar.copy(gate_c[:], gate_ps[:].rearrange("v i (d r) -> v i d r", d=D)[:, :, :, 0])
+        turn_even(1, up[1], False)
         scatter(2, 0, S)
-        leave_lo(1)
-        w01 = [bank(2 + a, [P, 2, CHUNK], F32, "w01_%d" % a) for a in range(2)]
+        round_even(1)
+        pair_ps = [bank(2 + a, [P, 2, CHUNK], F32, "pair_ps%d" % a) for a in range(2)]
         for a in range(2):
-            words = zt01[a][:].rearrange("q i s p -> q (i s p)").bitcast(F32)
+            words = even_t[a][:].rearrange("q i s p -> q (i s p)").bitcast(F32)
             for i in range(4):
-                turn(w01[a][:, i // 2, blk(i % 2)], words[:, blk(i)], True, True)
+                turn(pair_ps[a][:, i // 2, blk(i % 2)], words[:, blk(i)], True, True)
 
-        def place01(c):
+        def place_even(c):
             dst = zi[c][:].rearrange("p c t -> p (c t)").bitcast(F32).rearrange("p (c u) -> p c u", u=2)
-            nc.scalar.copy(dst, w01[c // 2][:, c % 2, :].unsqueeze(2).to_broadcast([P, CHUNK, 2]))
+            nc.scalar.copy(dst, pair_ps[c // 2][:, c % 2, :].unsqueeze(2).to_broadcast([P, CHUNK, 2]))
 
-        spans = ((2, 4), (4, 8))
-        t2 = [bank(7 - a, [P, (hi - lo) * P], F32, "t2_%d" % a) for a, (lo, hi) in enumerate(spans)]
-        place01(0)
-        place01(1)
-        for src, start in ((emb_t[2], True), (up[2], False)):
-            for a, (lo, hi) in enumerate(spans):
-                for i in range(lo, hi):
-                    turn(t2[a][:, blk(i - lo)], src[:, blk(i)], start and i == lo, not start and i == hi - 1)
+        odd_ps = bank(7, [P, 2 * CHUNK], F32, "odd_ps")
+        place_even(0)
+        place_even(1)
+        for src, opens in ((emb_t[2], True), (up[2], False)):
+            for i in range(4):
+                turn(odd_ps[:, blk(i)], src[:, blk(4 + i)], opens and i == 0, not opens and i == 3)
         scatter(3, 0, S)
-        zt2 = [sbuf([P, (hi - lo) * P], BF16, "zt2_%d" % a) for a, (lo, hi) in enumerate(spans)]
-        z2_ps = [bank(4 + a, [P, (hi - lo) * P], BF16, "z2_ps%d" % a) for a, (lo, hi) in enumerate(spans)]
-        place01(2)
+        odd_t = [sbuf([P, CHUNK], BF16, "odd_t%d" % a) for a in range(2)]
+        back_ps = [bank(4 + a, [P, CHUNK], BF16, "back_ps%d" % a) for a in range(2)]
+        place_even(2)
         for a in range(2):
-            nc.scalar.copy(zt2[a][:], t2[a][:])
-        for a, (lo, hi) in enumerate(spans):
-            for i in range(hi - lo):
-                nc.tensor.transpose(z2_ps[a][:, blk(i)], zt2[a][:, blk(i)], ident_b[:])
-        place01(3)
-        nc.scalar.copy(z23[1][:, 0, :], z2_ps[0][:])
-        for c in (2, 3):
-            nc.scalar.copy(z23[c][:, 0, :], z2_ps[1][:, cols(c - 2)])
+            nc.scalar.copy(odd_t[a][:], odd_ps[:, cols(a)])
+        for i in range(4):
+            nc.tensor.transpose(back_ps[i // 2][:, blk(i % 2)], odd_t[i // 2][:, blk(i % 2)], ident_b[:])
+        place_even(3)
+        for a in range(2):
+            nc.scalar.copy(z_odd[2 + a][:, 0, :], back_ps[a][:])
 
-        def add(s, c):
-            nc.vector.tensor_tensor(z23[c][:, s - 2, :], up[s][:, cols(c)], emb_t[s][:, cols(c)], ADD)
+        def add_emb(s, c):
+            nc.vector.tensor_tensor(z_odd[c][:, s - 2, :], up[s][:, cols(c)], emb_t[s][:, cols(c)], ADD)
 
-        def place23(c, copy):
-            copy(zi[c][:, :, 2:4], z23[c][:].rearrange("p e c -> p c e"))
+        def place_odd(c, copy):
+            copy(zi[c][:, :, 2:4], z_odd[c][:].rearrange("p e c -> p c e"))
 
         y = sbuf([P, U], F32, "y")
-        y_ps = [bank((5, 4, 2, 3)[c], [P, CHUNK], F32, "y_ps%d" % c) for c in range(chunks)]
+        y_ps = [bank((4 + c) if c < 2 else c, [P, CHUNK], F32, "y_ps%d" % c) for c in range(CHUNKS)]
 
-        def second(c):
-            codes, scales = quantize("zq%d" % c, zi[c][:].rearrange("p c t -> p (c t)"), CHUNK)
-            nc.tensor.matmul_mx(out=y_ps[c][:], lhsT=w2_q[0][:].bitcast(FP8X4), lhsT_scale=w2_q[1][:],
-                                rhs=codes[:].bitcast(FP8X4), rhs_scale=scales[:], start=True, stop=True)
+        def second_product(c):
+            tag = "odd_t%d" % c if c < 2 else None
+            codes, scales = quantize("zq%d" % c, zi[c][:].rearrange("p c t -> p (c t)"), CHUNK, tag)
+            nc.tensor.matmul_mx(
+                out=y_ps[c][:],
+                lhsT=w2_q[0][:].bitcast(FP8X4),
+                lhsT_scale=w2_q[1][:],
+                rhs=codes[:].bitcast(FP8X4),
+                rhs_scale=scales[:],
+                start=True,
+                stop=True,
+            )
 
-        add(2, 0)
-        for c in (1, 2, 0, 3):
-            add(3, c)
-        place23(0, nc.vector.tensor_copy)
-        for c in range(1, chunks):
-            place23(c, nc.scalar.copy)
-        for c in range(chunks):
-            second(c)
-        for c in range(chunks):
+        for s, c in ((2, 0), (3, 2), (3, 3), (3, 0), (2, 1), (3, 1)):
+            add_emb(s, c)
+        for c in range(CHUNKS):
+            place_odd(c, nc.vector.tensor_copy if c < 2 else nc.scalar.copy)
+        for c in range(CHUNKS):
+            second_product(c)
+        for c in range(CHUNKS):
             nc.scalar.activation(y[:, cols(c)], y_ps[c][:], RELU)
 
-        nblk = VA // P
+        blocks = VA // P
         got = [sbuf([P, VA], F32, "got%d" % d) for d in range(D)]
         scaled = [sbuf([P, VA], F32, "scaled%d" % d) for d in range(D)]
-        acc_ps = bank(6, [P, VA], F32, "acc_ps")
+        got_banks = ((4, 1, 2), (5, 7, 0))
+        acc_ps = [bank(6, [P, VA - P], F32, "acc_ps0"), bank(3, [P, P], F32, "acc_ps1")]
 
-        def back(d):
-            for i in range(nblk):
-                turn(acc_ps[:, blk(i)], scaled[d][:, blk(i)], d == 0 and i == 0, d == D - 1 and i == nblk - 1)
+        def turn_back(d):
+            for i in range(blocks):
+                opens, closes = d == 0 and i % 2 == 0, d == D - 1 and i > 0
+                turn(acc_ps[i // 2][:, blk(i % 2)], scaled[d][:, blk(i)], opens, closes)
 
         for d in range(D):
-            nc.vector.tensor_copy(got[d][:], y[:].indirect(pos_t[d][:, 0 : VA // 16]))
+            nc.vector.tensor_copy(got[d][:], y[:].indirect(pos_t[d][:, 0 : VA // LIST]))
             if d > 1:
-                back(d - 2)
-            got_ps = bank(4 + d % 2, [P, VA], F32, "got_ps%d" % d)
-            for i in range(nblk):
-                turn(got_ps[:, blk(i)], got[d][:, blk(i)], True, True)
-            for i in range(nblk):
-                nc.scalar.activation(scaled[d][:, blk(i)], got_ps[:, blk(i)], COPY, scale=gate_c[:, i, d : d + 1])
-        back(D - 2)
-        back(D - 1)
+                turn_back(d - 2)
+            for i in range(blocks):
+                got_ps = bank(got_banks[d % 2][i], [P, P], F32, "got_ps%d_%d" % (d, i))
+                turn(got_ps[:], got[d][:, blk(i)], True, True)
+                nc.scalar.activation(scaled[d][:, blk(i)], got_ps[:], COPY, scale=gate_c[:, i, d : d + 1])
+        turn_back(D - 2)
+        turn_back(D - 1)
         res_a = sbuf([P, VA], F32, "res_a")
-        nc.scalar.copy(res_a[:], acc_ps[:])
+        nc.scalar.copy(res_a[:, 0 : VA - P], acc_ps[0][:])
+        nc.scalar.copy(res_a[:, VA - P : VA], acc_ps[1][:])
         nc.sync.dma_start(out[:, 0:VA], res_a[:])
 
         prod = sbuf([P, D, VB], F32, "prod")
-        s01 = sbuf([P, VB], F32, "s01")
-        s012 = sbuf([P, VB], F32, "s012")
+        sum01 = sbuf([P, VB], F32, "sum01")
+        sum012 = sbuf([P, VB], F32, "sum012")
         res_b = sbuf([P, VB], F32, "res_b")
         for d in range(D):
-            nc.vector.tensor_tensor(prod[:, d, :], y[:].indirect(pos_t[d][:, VA // 16 : V // 16]), gate_b[:, d, :], MULT)
+            picked = y[:].indirect(pos_t[d][:, VA // LIST : V // LIST])
+            nc.vector.tensor_tensor(prod[:, d, :], picked, gate_b[:, d, :], MULT)
             if d == 2:
-                nc.vector.tensor_tensor(s01[:], prod[:, 0, :], prod[:, 1, :], ADD)
-        nc.vector.tensor_tensor(s012[:], s01[:], prod[:, 2, :], ADD)
-        nc.vector.tensor_tensor(res_b[:], s012[:], prod[:, 3, :], ADD)
+                nc.vector.tensor_tensor(sum01[:], prod[:, 0, :], prod[:, 1, :], ADD)
+        nc.vector.tensor_tensor(sum012[:], sum01[:], prod[:, 2, :], ADD)
+        nc.vector.tensor_tensor(res_b[:], sum012[:], prod[:, 3, :], ADD)
         nc.sync.dma_start(out[:, VA:V], res_b[:])

from contextlib import ExitStack

import concourse.mybir as mybir
from concourse.masks import make_identity

K, T, S, D, V, H, N, U = 512, 2048, 512, 4, 512, 512, 128, 1024
FLOPS = 2 * K * H * S + 2 * H * N * U

F32 = mybir.dt.float32
BF16 = mybir.dt.bfloat16
I32 = mybir.dt.int32
U32 = mybir.dt.uint32
U16 = mybir.dt.uint16
U8 = mybir.dt.uint8
FP8X4 = mybir.dt.float8_e4m3fn_x4
FP4X4 = mybir.dt.float4_e2m1fn_x4
COPY = mybir.ActivationFunctionType.Copy
RELU = mybir.ActivationFunctionType.Relu
ADD = mybir.AluOpType.add
MULT = mybir.AluOpType.mult

P = 128
PACK = 4
LIST = 16
CHUNK = 256
CHUNKS = U // CHUNK
VA = 3 * P
VB = V - VA


def tile_picked_devox_relu_p_kernel(
    tc, x_words, x_scales, w1, w2, gate, emb, offs, cell, pos1, pos2, pos3, pos4, out
):
    nc = tc.nc
    with ExitStack() as ctx:
        lists = ctx.enter_context(tc.tile_pool(name="lists", bufs=1))
        sb = ctx.enter_context(tc.tile_pool(name="sb", bufs=1))
        psum = ctx.enter_context(tc.psum_pool(name="psum", bufs=1))

        def sbuf(shape, dtype, name, tag=None):
            return sb.tile(shape, dtype, name=name, tag=tag or name, align_bytes=64)

        def bank(b, shape, dtype, name):
            return psum.tile(shape, dtype, name=name, tag="bank%d" % b)

        def load_list(src, name):
            tile = lists.tile([P, S // LIST], U16, name=name)
            nc.sync.dma_start(tile[:], src)
            return tile

        def blk(i):
            return slice(i * P, (i + 1) * P)

        def cols(c):
            return slice(c * CHUNK, (c + 1) * CHUNK)

        def quantize(name, src, width, tag=None):
            codes = sbuf([P, width], U32, name + "_c", tag)
            scales = sbuf([P, width], U8, name + "_s")
            nc.vector.quantize_mx(out=codes[:].bitcast(FP8X4), scales=scales[:], in_=src)
            return codes, scales

        xs_win = sbuf([P, T], U8, "xs_win")
        nc.gpsimd.memset(xs_win[:].bitcast(I32), 0)
        ident = sbuf([P, P], F32, "ident")
        make_identity(nc, ident[:])
        ident_b = sbuf([P, P], BF16, "ident_b")
        nc.scalar.copy(ident_b[:], ident[:])
        up = [sbuf([P, U], F32, "up%d" % s) for s in range(PACK)]
        for s in range(PACK - 1):
            nc.vector.memset(up[s][:], 0.0)
        nc.scalar.copy(up[PACK - 1][:], up[0][:])

        def turn(dst, src, start, stop):
            nc.tensor.matmul(dst, src, ident[:], start=start, stop=stop, is_transpose=True)

        xw_win = sbuf([P, T], U16, "xw_win")
        nc.sync.dma_start(xw_win[:].bitcast(I32), x_words[0].bitcast(I32))
        offs_t = load_list(offs, "offs_t")
        for q in range(4):
            nc.sync.dma_start(
                xs_win[32 * q : 32 * q + 4, :].bitcast(I32), x_scales[0, 4 * q : 4 * q + 4, :].bitcast(I32)
            )
        w1_rows = w1.rearrange("(p t) c -> p t c", t=PACK)
        w1_raw = [sbuf([P, PACK, H // 2], F32, "w1_raw%d" % a) for a in range(2)]
        for a in range(2):
            nc.sync.dma_start(w1_raw[a][:], w1_rows[:, :, a * (H // 2) : (a + 1) * (H // 2)])
        cell_t = load_list(cell, "cell_t")
        emb_even = emb.rearrange("(s q e) c -> e s q c", s=2, e=2)[0]
        emb_fourth = emb.rearrange("(p f) c -> f p c", f=PACK)
        emb_t = [sbuf([P, U], F32, "emb%d" % s) for s in range(PACK)]
        w2_raw = sbuf([P, PACK, N], F32, "w2_raw")
        for s in range(2):
            nc.sync.dma_start(emb_t[s][:], emb_even[s])
        nc.sync.dma_start(w2_raw[:], w2.rearrange("(p f) n -> p f n", f=PACK))
        for s in range(2, PACK):
            nc.sync.dma_start(emb_t[s][:], emb_fourth[2 * s - 3])
        pos_t = [load_list(src, "pos%d_t" % d) for d, src in enumerate((pos1, pos2, pos3, pos4))]
        gate_a = sbuf([P, VA], F32, "gate_a")
        nc.sync.dma_start(gate_a[:], gate.rearrange("d (r f) v -> f (d r) v", f=D)[0, :, 0:VA])
        gate_b = sbuf([P, D, VB], F32, "gate_b")
        nc.sync.dma_start(gate_b[:], gate[:, :, VA:V].rearrange("d p v -> p d v"))

        xw = sbuf([P, S], U16, "xw")
        xs = sbuf([P, S], U8, "xs")
        nc.vector.tensor_copy(xw[:], xw_win[:].indirect(offs_t[:]))
        nc.vector.tensor_copy(xs[:], xs_win[:].indirect(offs_t[:]))

        w1_even = [sbuf([P, P * PACK], BF16, "w1_even%d" % s) for s in range(2)]
        w1_odd = sbuf([P, 2, P * PACK], BF16, "w1_odd")
        h_ps = [bank(b, [P, S], F32, "h_ps%d" % b) for b in range(PACK)]
        h = [sbuf([P, S], F32, "h%d" % s) for s in range(PACK)]

        def cast_even(s):
            dst = w1_even[s][:].rearrange("p (q t) -> p q t", t=PACK)
            src = w1_raw[s][:].rearrange("p t (q e) -> p e q t", e=2)[:, 0]
            for q in (0, P // 2):
                nc.scalar.copy(dst[:, q : q + P // 2], src[:, q : q + P // 2])

        def cast_odd(a):
            dst = w1_odd[:].rearrange("p s (m t) -> p m s t", t=PACK)[:, a * P // 2 : (a + 1) * P // 2]
            src = w1_raw[a][:].rearrange("p t (m s e) -> p e m s t", s=2, e=2)[:, 1]
            for m in (0, P // 4):
                nc.scalar.copy(dst[:, m : m + P // 4], src[:, m : m + P // 4])

        def first_product(s, b, lo, hi):
            codes, scales = w1_q[s]
            nc.tensor.matmul_mx(
                out=h_ps[b][:, lo:hi],
                lhsT=codes.bitcast(FP8X4),
                lhsT_scale=scales,
                rhs=xw[:, lo:hi].bitcast(FP4X4),
                rhs_scale=xs[:, lo:hi],
                start=True,
                stop=True,
            )
            nc.scalar.activation(h[s][:, lo:hi], h_ps[b][:, lo:hi], RELU)

        def scatter(s, lo, hi):
            nc.vector.tensor_copy(up[s][:].indirect(cell_t[:, lo // LIST : hi // LIST]), h[s][:, lo:hi])

        cast_even(0)
        codes, scales = quantize("w1q0", w1_even[0][:], P)
        w1_q = [(codes[:], scales[:])]
        first_product(0, 0, 0, S // 2)
        scatter(0, 0, S // 2)
        cast_even(1)
        for a in range(2):
            cast_odd(a)
        codes, scales = quantize("w1q1", w1_even[1][:], P)
        w1_q.append((codes[:], scales[:]))
        codes, scales = quantize("w1q23", w1_odd[:].rearrange("p s c -> p (s c)"), 2 * P)
        w1_q.extend((codes[:, blk(s)], scales[:, blk(s)]) for s in range(2))
        first_product(0, 1, S // 2, S)
        scatter(0, S // 2, S)
        for s in range(1, PACK):
            first_product(s, (s + 1) % PACK, 0, S)
        scatter(1, 0, S)

        w2_b = sbuf([P, N * PACK], BF16, "w2_b")
        nc.scalar.copy(
            w2_b[:].rearrange("p (n u e) -> p n u e", u=2, e=2), w2_raw[:].rearrange("p (e u) n -> p n u e", u=2)
        )
        w2_q = quantize("w2q", w2_b[:], N)

        z_odd = [sbuf([P, 2, CHUNK], BF16, "z_odd%d" % c) for c in range(CHUNKS)]
        zi = [sbuf([P, CHUNK, PACK], BF16, "zi%d" % c) for c in range(CHUNKS)]

        even_ps = [[bank(4 + 2 * s + a, [P, 4, P], F32, "even_ps%d_%d" % (s, a)) for a in range(2)] for s in range(2)]
        even_t = [sbuf([P, 4, 2, P], BF16, "even_t%d" % a) for a in range(2)]

        def turn_even(s, src, opens):
            for a in range(2):
                for i in range(4):
                    turn(even_ps[s][a][:, i, :], src[:, blk(4 * a + i)], opens and i == 0, not opens and i == 3)

        def round_even(s):
            for a in range(2):
                nc.scalar.copy(even_t[a][:, :, s, :], even_ps[s][a][:])

        turn_even(0, emb_t[0], True)
        turn_even(1, emb_t[1], True)
        turn_even(0, up[0], False)
        gate_ps = bank(1, [P, VA // P, P], F32, "gate_ps")
        for i in range(VA // P):
            turn(gate_ps[:, i, :], gate_a[:, blk(i)], True, True)
        round_even(0)
        gate_c = sbuf([P, VA // P, D], F32, "gate_c")
        nc.scalar.copy(gate_c[:], gate_ps[:].rearrange("v i (d r) -> v i d r", d=D)[:, :, :, 0])
        turn_even(1, up[1], False)
        scatter(2, 0, S)
        round_even(1)
        pair_ps = [bank(2 + a, [P, 2, CHUNK], F32, "pair_ps%d" % a) for a in range(2)]
        for a in range(2):
            words = even_t[a][:].rearrange("q i s p -> q (i s p)").bitcast(F32)
            for i in range(4):
                turn(pair_ps[a][:, i // 2, blk(i % 2)], words[:, blk(i)], True, True)

        def place_even(c):
            dst = zi[c][:].rearrange("p c t -> p (c t)").bitcast(F32).rearrange("p (c u) -> p c u", u=2)
            nc.scalar.copy(dst, pair_ps[c // 2][:, c % 2, :].unsqueeze(2).to_broadcast([P, CHUNK, 2]))

        odd_ps = bank(7, [P, 2 * CHUNK], F32, "odd_ps")
        place_even(0)
        place_even(1)
        for src, opens in ((emb_t[2], True), (up[2], False)):
            for i in range(4):
                turn(odd_ps[:, blk(i)], src[:, blk(4 + i)], opens and i == 0, not opens and i == 3)
        scatter(3, 0, S)
        odd_t = [sbuf([P, CHUNK], BF16, "odd_t%d" % a) for a in range(2)]
        back_ps = [bank(4 + a, [P, CHUNK], BF16, "back_ps%d" % a) for a in range(2)]
        place_even(2)
        for a in range(2):
            nc.scalar.copy(odd_t[a][:], odd_ps[:, cols(a)])
        for i in range(4):
            nc.tensor.transpose(back_ps[i // 2][:, blk(i % 2)], odd_t[i // 2][:, blk(i % 2)], ident_b[:])
        place_even(3)
        for a in range(2):
            nc.scalar.copy(z_odd[2 + a][:, 0, :], back_ps[a][:])

        def add_emb(s, c):
            nc.vector.tensor_tensor(z_odd[c][:, s - 2, :], up[s][:, cols(c)], emb_t[s][:, cols(c)], ADD)

        def place_odd(c, copy):
            copy(zi[c][:, :, 2:4], z_odd[c][:].rearrange("p e c -> p c e"))

        y = sbuf([P, U], F32, "y")
        y_ps = [bank((4 + c) if c < 2 else c, [P, CHUNK], F32, "y_ps%d" % c) for c in range(CHUNKS)]

        def second_product(c):
            tag = "odd_t%d" % c if c < 2 else None
            codes, scales = quantize("zq%d" % c, zi[c][:].rearrange("p c t -> p (c t)"), CHUNK, tag)
            nc.tensor.matmul_mx(
                out=y_ps[c][:],
                lhsT=w2_q[0][:].bitcast(FP8X4),
                lhsT_scale=w2_q[1][:],
                rhs=codes[:].bitcast(FP8X4),
                rhs_scale=scales[:],
                start=True,
                stop=True,
            )

        for s, c in ((2, 0), (3, 2), (3, 3), (3, 0), (2, 1), (3, 1)):
            add_emb(s, c)
        for c in range(CHUNKS):
            place_odd(c, nc.vector.tensor_copy if c < 2 else nc.scalar.copy)
        for c in range(CHUNKS):
            second_product(c)
        for c in range(CHUNKS):
            nc.scalar.activation(y[:, cols(c)], y_ps[c][:], RELU)

        blocks = VA // P
        got = [sbuf([P, VA], F32, "got%d" % d) for d in range(D)]
        scaled = [sbuf([P, VA], F32, "scaled%d" % d) for d in range(D)]
        got_banks = ((4, 1, 2), (5, 7, 0))
        acc_ps = [bank(6, [P, VA - P], F32, "acc_ps0"), bank(3, [P, P], F32, "acc_ps1")]

        def turn_back(d):
            for i in range(blocks):
                opens, closes = d == 0 and i % 2 == 0, d == D - 1 and i > 0
                turn(acc_ps[i // 2][:, blk(i % 2)], scaled[d][:, blk(i)], opens, closes)

        for d in range(D):
            nc.vector.tensor_copy(got[d][:], y[:].indirect(pos_t[d][:, 0 : VA // LIST]))
            if d > 1:
                turn_back(d - 2)
            for i in range(blocks):
                got_ps = bank(got_banks[d % 2][i], [P, P], F32, "got_ps%d_%d" % (d, i))
                turn(got_ps[:], got[d][:, blk(i)], True, True)
                nc.scalar.activation(scaled[d][:, blk(i)], got_ps[:], COPY, scale=gate_c[:, i, d : d + 1])
        turn_back(D - 2)
        turn_back(D - 1)
        res_a = sbuf([P, VA], F32, "res_a")
        nc.scalar.copy(res_a[:, 0 : VA - P], acc_ps[0][:])
        nc.scalar.copy(res_a[:, VA - P : VA], acc_ps[1][:])
        nc.sync.dma_start(out[:, 0:VA], res_a[:])

        prod = sbuf([P, D, VB], F32, "prod")
        sum01 = sbuf([P, VB], F32, "sum01")
        sum012 = sbuf([P, VB], F32, "sum012")
        res_b = sbuf([P, VB], F32, "res_b")
        for d in range(D):
            picked = y[:].indirect(pos_t[d][:, VA // LIST : V // LIST])
            nc.vector.tensor_tensor(prod[:, d, :], picked, gate_b[:, d, :], MULT)
            if d == 2:
                nc.vector.tensor_tensor(sum01[:], prod[:, 0, :], prod[:, 1, :], ADD)
        nc.vector.tensor_tensor(sum012[:], sum01[:], prod[:, 2, :], ADD)
        nc.vector.tensor_tensor(res_b[:], sum012[:], prod[:, 3, :], ADD)
        nc.sync.dma_start(out[:, VA:V], res_b[:])
